import numpy as np
import ml_dtypes


def mxq(x, axis, fmt="e4m3"):
    dtype, down = {"e4m3": (ml_dtypes.float8_e4m3fn, 7), "e5m2": (ml_dtypes.float8_e5m2, 14)}[fmt]
    v = np.moveaxis(np.asarray(x, np.float32).astype(ml_dtypes.bfloat16).astype(np.float64), axis, -1)
    blocks = v.reshape(v.shape[:-1] + (-1, 32))
    amax = np.abs(blocks).max(-1, keepdims=True)
    byte = np.maximum(np.where(amax > 0, np.frexp(amax)[1] - 1 + 127, 0) - down, 1)
    scale = np.exp2(byte - 127.0)
    codes = (blocks / scale).astype(np.float32).astype(dtype).astype(np.float64)
    return np.moveaxis((codes * scale).reshape(v.shape), -1, axis)


WIDE = False


def mx_kscale(k):
    if not WIDE:
        return np.ones(k)
    levels = np.array([10, -10, 5, -5, 0])
    if k % 512:
        return np.exp2(np.random.permutation(np.resize(levels, k // 32))).repeat(32)
    a = np.empty((k // 512, 16))
    for p in range(k // 512):
        a[p, :8] = np.random.permutation(np.resize(levels, 8))
        for g in range(8):
            far = levels[np.abs(levels - a[p, g]) >= 10]
            a[p, g + 8] = far[np.random.randint(len(far))]
    return np.exp2(a.ravel()).repeat(32)


def f64(x):
    return np.asarray(x).astype(np.float64)


def striped(idx):
    return np.tile(idx.reshape(-1, 16).T, (8, 1)).astype(np.uint16)


def unstriped(offs):
    return offs[:16].T.reshape(-1).astype(np.int64)


def striped8(idx):
    return np.concatenate([x.reshape(-1, 16).T for x in idx]).astype(np.uint16)


def runs(offs, k):
    lists = np.stack([offs[16 * r : 16 * r + 16].T.reshape(-1) for r in range(8)]).astype(np.int64)
    return lists[np.arange(k) % 512 // 64]


def pack_weight(w):
    k, n = w.shape
    w = f64(np.asarray(w, np.float32).astype(ml_dtypes.bfloat16)).reshape(k // 32, 32, n)
    amax = np.abs(w).max(1)
    byte = np.clip(np.where(amax > 0, np.frexp(amax)[1] - 1 + 127 - 7, 1), 1, 254)
    scaled = (w * np.exp2(127.0 - byte)[:, None, :]).reshape(k, n).astype(np.float32)
    words = np.ascontiguousarray(scaled.reshape(k // 512, 128, 4, n).transpose(0, 1, 3, 2)).astype(ml_dtypes.float8_e4m3fn).view(np.uint8)
    return words, np.ascontiguousarray(byte.astype(np.uint8).reshape(k // 512, 16, n))


def unpack_weight(words, scales):
    g, p, n, _ = words.shape
    vals = np.ascontiguousarray(words).view(ml_dtypes.float8_e4m3fn).astype(np.float64) * np.repeat(np.exp2(scales.astype(np.float64) - 127.0), 8, axis=1)[..., None]
    return vals.transpose(0, 1, 3, 2).reshape(g * 512, n)


def sigmoid(v):
    return 1.0 / (1.0 + np.exp(-np.maximum(v, -700.0)))


K, T, S, H, C = 512, 2048, 512, 512, 512


def setup_inputs():
    n = np.random.standard_normal
    s = mx_kscale(K)[:, None]
    packed_xT = pack_weight(n((K, T)) * s)
    return {
        "x_words": packed_xT[0],
        "x_scales": packed_xT[1],
        "w1": (n((K, H)) / np.sqrt(K) / s).astype(np.float32),
        "gs": (np.random.uniform(0.5, 1.5, (K, 1)) / s).astype(np.float32),
        "gs2": (np.random.uniform(0.5, 1.5, (K, 1)) / s).astype(np.float32),
        "offs": striped(np.random.permutation(T)[:S]),
        "n1": striped(np.random.permutation(S)),
        "n2": striped(np.random.permutation(S)),
        "n3": striped8(np.stack([np.random.permutation(S) for _ in range(8)])),
        "n4": striped8(np.stack([np.random.permutation(S) for _ in range(8)])),
        "ca": striped(np.random.permutation(T)[:C]),
        "cb": striped(np.random.permutation(T)[:C]),
        "n5": striped8(np.stack([np.random.permutation(S) for _ in range(8)])),
        "n6": striped8(np.stack([np.random.permutation(S) for _ in range(8)])),
    }


def reference(x_words, x_scales, w1, gs, gs2, offs, n1, n2, n3, n4, ca, cb, n5, n6):
    x_ca = unpack_weight(x_words, x_scales)[:, unstriped(ca)]
    xq = unpack_weight(x_words, x_scales)[:, unstriped(offs)]
    y = mxq(f64(w1), 0, "e4m3").T @ xq
    st = y + 0.5 * y[:, unstriped(n1)]
    z = f64(gs) * (st - st[:, unstriped(n2)])
    a = 0.0625 * ((x_ca.T @ mxq(z, 0, "e4m3")))
    x_cb = unpack_weight(x_words, x_scales)[:, unstriped(cb)]
    pa = y[np.arange(H)[:, None], runs(n3, H)]
    pb = y[np.arange(H)[:, None], runs(n4, H)]
    z2 = f64(gs2) * (np.maximum(np.minimum(y, pa), np.minimum(np.maximum(y, pa), pb)))
    b = 0.0625 * ((x_cb.T @ mxq(z2, 0, "e4m3")))
    return (a + a[np.arange(C)[:, None], runs(n5, C)]) * (sigmoid(b + b[np.arange(C)[:, None], runs(n6, C)]))

@@ -1,0 +1,202 @@
+from contextlib import ExitStack
+
+import concourse.mybir as mybir
+from concourse.masks import make_identity
+
+K, T, S = 512, 2048, 512
+FLOPS = 3 * 2 * K * S * S
+
+F32 = mybir.dt.float32
+BF16 = mybir.dt.bfloat16
+I32 = mybir.dt.int32
+U32 = mybir.dt.uint32
+U16 = mybir.dt.uint16
+U8 = mybir.dt.uint8
+FP8X4 = mybir.dt.float8_e4m3fn_x4
+ALU = mybir.AluOpType
+ACT = mybir.ActivationFunctionType
+
+P = 128
+PACK = 4
+HALF = S // 2
+
+
+def tile_picked_twocdtriebhopmed_none_p_kernel(tc, x_words, x_scales, w1, gs, gs2, offs, n1, n2, n3, n4, ca, cb, n5, n6, out):
+    nc = tc.nc
+    with ExitStack() as ctx:
+        lists = ctx.enter_context(tc.tile_pool(name="lists", bufs=1))
+        keep = ctx.enter_context(tc.tile_pool(name="keep", bufs=1))
+        psum = ctx.enter_context(tc.psum_pool(name="psum", bufs=1))
+
+        def load_list(name, src):
+            tile = lists.tile([P, S // 16], U16, name=name)
+            nc.sync.dma_start(tile[:], src)
+            return tile
+
+        def tiles(name, dtype, width=S):
+            return [keep.tile([P, width], dtype, name="%s%d" % (name, t), align_bytes=64) for t in range(PACK)]
+
+        def plane(tile, t):
+            return tile[:, t * S : (t + 1) * S]
+
+        x_bytes = keep.tile([P, T], U8, name="x_bytes", align_bytes=64)
+        nc.vector.memset(x_bytes[:].bitcast(I32), 0)
+        w_rows = w1.rearrange("(p j) c -> p j c", j=PACK)
+        w_raw = [keep.tile([P, PACK, HALF], F32, name="w_raw%d" % h) for h in range(2)]
+        nc.sync.dma_start(w_raw[0][:], w_rows[:, :, :HALF])
+        for q in range(4):
+            nc.sync.dma_start(x_bytes[32 * q : 32 * q + 4, :].bitcast(I32), x_scales[0, 4 * q : 4 * q + 4, :].bitcast(I32))
+        offs_l = load_list("offs_l", offs)
+        nc.sync.dma_start(w_raw[1][:], w_rows[:, :, HALF:])
+        x_codes = keep.tile([P, T], U32, name="x_codes", align_bytes=64)
+        nc.sync.dma_start(x_codes[:].bitcast(I32), x_words[0].rearrange("p n t -> p (n t)").bitcast(I32))
+        cb_l = load_list("cb_l", cb)
+        gain2 = keep.tile([P, PACK], F32, name="gain2")
+        nc.sync.dma_start(gain2[:], gs2.rearrange("(p t) o -> p (t o)", t=PACK))
+        n4_l = load_list("n4_l", n4)
+        n3_l = load_list("n3_l", n3)
+        ca_l = load_list("ca_l", ca)
+        gain1 = keep.tile([P, PACK], F32, name="gain1")
+        nc.sync.dma_start(gain1[:], gs.rearrange("(p t) o -> p (t o)", t=PACK))
+        n1_l = load_list("n1_l", n1)
+        n2_l = load_list("n2_l", n2)
+        n6_l = load_list("n6_l", n6)
+        n5_l = load_list("n5_l", n5)
+
+        def pick(name, table, offsets, dealt, tag=None):
+            dst = keep.tile([P, S], table.dtype, name=name, tag=tag or name, align_bytes=64)
+            view = dst[:].rearrange("p (t m) -> p m t", t=PACK) if dealt else dst[:]
+            nc.vector.tensor_copy(view, table[:].indirect(offsets[:]))
+            return dst
+
+        def fetch(engine, dst, window, offsets, scale=1.0):
+            for h in range(2):
+                src = window.indirect(offsets[:, h * (HALF // 16) : (h + 1) * (HALF // 16)])
+                if engine == "scalar":
+                    nc.scalar.activation(dst[:, h * HALF : (h + 1) * HALF], src, ACT.Copy, scale=scale)
+                else:
+                    nc.vector.tensor_copy(dst[:, h * HALF : (h + 1) * HALF], src)
+
+        def drain(engine, dst, bank, scale):
+            if engine == "scalar":
+                nc.scalar.activation(dst, bank, ACT.Copy, scale=scale)
+            else:
+                nc.vector.tensor_scalar(dst, bank, scale, None, ALU.mult)
+
+        def add(engine, dst, left, right):
+            (nc.vector if engine == "vector" else nc.gpsimd).tensor_tensor(dst, left, right, ALU.add)
+
+        def product(bank, cols, lhs, t, rhs):
+            m = slice(t * P, (t + 1) * P)
+            nc.tensor.matmul_mx(
+                out=bank[:, cols], lhsT=lhs[0][:, m].bitcast(FP8X4), lhsT_scale=lhs[1][:, m],
+                rhs=rhs[0][:].bitcast(FP8X4), rhs_scale=rhs[1][:], start=True, stop=True,
+            )
+
+        def weave(name, left, right, op):
+            woven = []
+            for h in range(2):
+                dst = keep.tile([P, HALF * PACK], BF16, name="%s_woven%d" % (name, h), tag="%s_woven%d" % (name, h), align_bytes=64)
+                views = [
+                    src[:].rearrange("p (t s) -> p t s", t=PACK)[:, :, h * HALF : (h + 1) * HALF].rearrange("p t (c i) -> p c t i", i=2)
+                    for src in (left, right)
+                ]
+                nc.vector.tensor_tensor(dst[:].rearrange("p (c i t) -> p c t i", i=2, t=PACK), views[0], views[1], op)
+                woven.append(dst)
+            packed = []
+            for h in range(2):
+                codes = keep.tile([P, HALF], U32, name="%s_codes%d" % (name, h), align_bytes=64)
+                scales = keep.tile([P, HALF], U8, name="%s_scales%d" % (name, h), align_bytes=64)
+                nc.vector.quantize_mx(out=codes[:].bitcast(FP8X4), scales=scales[:], in_=woven[h][:])
+                packed.append((codes, scales))
+            return packed
+
+        ident = keep.tile([P, P], F32, name="ident")
+        make_identity(nc, ident[:])
+        w_bf = keep.tile([P, PACK * S], BF16, name="w_bf", align_bytes=64)
+        w_view = w_bf[:].rearrange("p (t m j) -> p m t j", t=PACK, j=PACK)
+        for h, copy in enumerate((nc.vector.tensor_copy, nc.scalar.copy)):
+            copy(w_view[:, h * P // 2 : (h + 1) * P // 2], w_raw[h][:].rearrange("p j (m t) -> p m t j", t=PACK))
+        xq_scales = pick("xq_scales", x_bytes, offs_l, False)
+        w_codes = keep.tile([P, S], U32, name="w_codes", align_bytes=64)
+        w_scales = keep.tile([P, S], U8, name="w_scales", align_bytes=64)
+        nc.vector.quantize_mx(out=w_codes[:].bitcast(FP8X4), scales=w_scales[:], in_=w_bf[:])
+        xq = (pick("xq_codes", x_codes, offs_l, False), xq_scales)
+        y_banks = [psum.tile([P, S], F32, name="y_bank%d" % t, tag="bank%d" % t) for t in range(PACK)]
+        for t in range(PACK):
+            product(y_banks[t], slice(0, S), (w_codes, w_scales), t, xq)
+        xb_scales = pick("xb_scales", x_bytes, cb_l, True, tag="xq_scales")
+        xb = (pick("xb_codes", x_codes, cb_l, True), xb_scales)
+
+        y2 = tiles("y2", F32)
+        pa = tiles("pa", BF16)
+        pb = tiles("pb", BF16)
+        hi = tiles("hi", BF16)
+        lo = keep.tile([P, PACK * S], BF16, name="lo", align_bytes=64)
+        mid = keep.tile([P, PACK * S], BF16, name="mid", align_bytes=64)
+        for t in range(PACK):
+            drain(("scalar", "scalar", "scalar", "scalar")[t], y2[t][:], y_banks[t][:], gain2[:, t : t + 1])
+            fetch("scalar", pb[t], y2[t][:], n4_l)
+            fetch(("vector", "vector", "vector", "scalar")[t], pa[t], y2[t][:], n3_l)
+            nc.vector.tensor_tensor(hi[t][:], pa[t][:], pb[t][:], ALU.max)
+            nc.vector.tensor_tensor(plane(lo, t), pa[t][:], pb[t][:], ALU.min)
+            nc.vector.tensor_tensor(plane(mid, t), hi[t][:], y2[t][:], ALU.min)
+        z2 = weave("z2", lo, mid, ALU.max)
+        b_banks = [psum.tile([P, S], F32, name="b_bank%d" % t, tag="bank%d" % (PACK + t)) for t in range(PACK)]
+        for t in range(PACK):
+            for h in range(2):
+                product(b_banks[t], slice(h * HALF, (h + 1) * HALF), xb, t, z2[h])
+
+        y1 = tiles("y1", F32)
+        g1 = tiles("g1", F32)
+        st = keep.tile([P, PACK * S], F32, name="st", align_bytes=64)
+        g2 = keep.tile([P, PACK * S], F32, name="g2", align_bytes=64)
+        for t in range(PACK):
+            drain(("scalar", "scalar", "scalar", "scalar")[t], y1[t][:], y_banks[t][:], gain1[:, t : t + 1])
+            fetch("scalar", g1[t], y1[t][:], n1_l, scale=0.5)
+            add(("vector", "vector", "vector", "vector")[t], plane(st, t), y1[t][:], g1[t][:])
+        b = tiles("b", F32)
+        for t in range(PACK):
+            drain(("scalar", "scalar", "scalar", "scalar")[t], b[t][:], b_banks[t][:], 0.03125)
+        for t in range(PACK):
+            fetch(("vector", "vector", "scalar", "scalar")[t], plane(g2, t), plane(st, t), n2_l)
+        xa = (pick("xa_codes", x_codes, ca_l, True, tag="z2_woven1"), pick("xa_scales", x_bytes, ca_l, True, tag="xq_scales"))
+        z = weave("z", st, g2, ALU.subtract)
+        a_banks = [psum.tile([P, S], F32, name="a_bank%d" % t, tag="bank%d" % t) for t in range(PACK)]
+        for t in range(PACK):
+            for h in range(2):
+                product(a_banks[t], slice(h * HALF, (h + 1) * HALF), xa, t, z[h])
+
+        g6 = tiles("g6", F32)[: PACK - 1] + [keep.tile([P, S], F32, name="g6_last", tag="z_woven1", align_bytes=64)]
+        th = tiles("th", F32)
+        a = tiles("a", F32)
+        g5 = tiles("g5", F32)
+        v = tiles("v", F32)
+        res = tiles("res", F32)
+        gates = []
+        out_rows = out.rearrange("(p t) s -> p t s", t=PACK)
+        blocks = [slice(c * P, (c + 1) * P) for c in range(S // P)]
+
+        def gate_of(t, engine):
+            fetch(engine, g6[t], b[t][:], n6_l)
+            turned = psum.tile([P, S], F32, name="turned%d" % t, tag="bank%d" % (PACK + t))
+            for cols in blocks:
+                nc.tensor.matmul(turned[:, cols], lhsT=b[t][:, cols], rhs=ident[:], is_transpose=True, start=True, stop=False)
+                nc.tensor.matmul(turned[:, cols], lhsT=g6[t][:, cols], rhs=ident[:], is_transpose=True, start=False, stop=True)
+            nc.scalar.activation(th[t][:], turned[:], ACT.Tanh)
+            gate = psum.tile([P, S], F32, name="gate%d" % t, tag="bank%d" % (PACK + t))
+            for cols in blocks:
+                nc.tensor.transpose(gate[:, cols], th[t][:, cols], ident[:])
+            gates.append(gate)
+
+        for t in range(PACK - 1):
+            gate_of(t, ("scalar", "scalar", "scalar", "vector")[t])
+        for t in range(PACK):
+            drain(("vector", "vector", "vector", "vector")[t], a[t][:], a_banks[t][:], 0.03125)
+        gate_of(PACK - 1, ("scalar", "scalar", "scalar", "vector")[PACK - 1])
+        for t in range(PACK):
+            fetch("scalar", g5[t], a[t][:], n5_l)
+            for cols in ([slice(0, S)] if t < PACK - 1 else [slice(0, HALF), slice(HALF, S)]):
+                add(("vector", "vector", "vector", "vector")[t], v[t][:, cols], a[t][:, cols], g5[t][:, cols])
+                nc.vector.scalar_tensor_tensor(res[t][:, cols], gates[t][:, cols], 1.0, v[t][:, cols], ALU.add, ALU.mult)
+                nc.sync.dma_start(out_rows[:, t, cols], res[t][:, cols])

@@ -1,7 +1,6 @@
 from contextlib import ExitStack
 
 import concourse.mybir as mybir
-from concourse.masks import make_identity
 
 K, T, S = 512, 2048, 512
 FLOPS = 3 * 2 * K * S * S
@@ -19,6 +18,10 @@ ACT = mybir.ActivationFunctionType
 P = 128
 PACK = 4
 HALF = S // 2
+GROUP = 16
+N6_ON_SCALAR = 2
+A_OUT_ON_SCALAR = 1
+SCORE_SCALE = 0.0625 * 0.5
 
 
 def tile_picked_twocdtriebhopmed_none_p_kernel(tc, x_words, x_scales, w1, gs, gs2, offs, n1, n2, n3, n4, ca, cb, n5, n6, out):
@@ -28,18 +31,26 @@ def tile_picked_twocdtriebhopmed_none_p_kernel(tc, x_words, x_scales, w1, gs, gs
         keep = ctx.enter_context(tc.tile_pool(name="keep", bufs=1))
         psum = ctx.enter_context(tc.psum_pool(name="psum", bufs=1))
 
+        def sbuf(name, width, dtype, tag=None):
+            return keep.tile([P, width], dtype, name=name, tag=tag or name, align_bytes=64)
+
+        def four(name, dtype, tags=None):
+            return [sbuf("%s%d" % (name, t), S, dtype, (tags or {}).get(t)) for t in range(PACK)]
+
+        def part(tile, t):
+            return tile[:, t * S : (t + 1) * S]
+
         def load_list(name, src):
-            tile = lists.tile([P, S // 16], U16, name=name)
+            tile = lists.tile([P, S // GROUP], U16, name=name)
             nc.sync.dma_start(tile[:], src)
             return tile
 
-        def tiles(name, dtype, width=S):
-            return [keep.tile([P, width], dtype, name="%s%d" % (name, t), align_bytes=64) for t in range(PACK)]
+        def load_gain(name, src):
+            tile = sbuf(name, PACK, F32)
+            nc.sync.dma_start(tile[:], src.rearrange("(p t) o -> p (t o)", t=PACK))
+            return tile
 
-        def plane(tile, t):
-            return tile[:, t * S : (t + 1) * S]
-
-        x_bytes = keep.tile([P, T], U8, name="x_bytes", align_bytes=64)
+        x_bytes = sbuf("x_bytes", T, U8)
         nc.vector.memset(x_bytes[:].bitcast(I32), 0)
         w_rows = w1.rearrange("(p j) c -> p j c", j=PACK)
         w_raw = [keep.tile([P, PACK, HALF], F32, name="w_raw%d" % h) for h in range(2)]
@@ -48,155 +59,129 @@ def tile_picked_twocdtriebhopmed_none_p_kernel(tc, x_words, x_scales, w1, gs, gs
             nc.sync.dma_start(x_bytes[32 * q : 32 * q + 4, :].bitcast(I32), x_scales[0, 4 * q : 4 * q + 4, :].bitcast(I32))
         offs_l = load_list("offs_l", offs)
         nc.sync.dma_start(w_raw[1][:], w_rows[:, :, HALF:])
-        x_codes = keep.tile([P, T], U32, name="x_codes", align_bytes=64)
+        x_codes = sbuf("x_codes", T, U32)
         nc.sync.dma_start(x_codes[:].bitcast(I32), x_words[0].rearrange("p n t -> p (n t)").bitcast(I32))
         cb_l = load_list("cb_l", cb)
-        gain2 = keep.tile([P, PACK], F32, name="gain2")
-        nc.sync.dma_start(gain2[:], gs2.rearrange("(p t) o -> p (t o)", t=PACK))
-        n4_l = load_list("n4_l", n4)
-        n3_l = load_list("n3_l", n3)
-        ca_l = load_list("ca_l", ca)
-        gain1 = keep.tile([P, PACK], F32, name="gain1")
-        nc.sync.dma_start(gain1[:], gs.rearrange("(p t) o -> p (t o)", t=PACK))
+        gain1 = load_gain("gain1", gs)
         n1_l = load_list("n1_l", n1)
+        gain2 = load_gain("gain2", gs2)
+        n3_l = load_list("n3_l", n3)
+        n4_l = load_list("n4_l", n4)
         n2_l = load_list("n2_l", n2)
+        ca_l = load_list("ca_l", ca)
         n6_l = load_list("n6_l", n6)
         n5_l = load_list("n5_l", n5)
 
         def pick(name, table, offsets, dealt, tag=None):
-            dst = keep.tile([P, S], table.dtype, name=name, tag=tag or name, align_bytes=64)
+            dst = sbuf(name, S, table.dtype, tag)
             view = dst[:].rearrange("p (t m) -> p m t", t=PACK) if dealt else dst[:]
             nc.vector.tensor_copy(view, table[:].indirect(offsets[:]))
             return dst
 
-        def fetch(engine, dst, window, offsets, scale=1.0):
+        def fetch(on_scalar, dst, window, offsets, scale=1.0):
             for h in range(2):
-                src = window.indirect(offsets[:, h * (HALF // 16) : (h + 1) * (HALF // 16)])
-                if engine == "scalar":
+                src = window.indirect(offsets[:, h * HALF // GROUP : (h + 1) * HALF // GROUP])
+                if on_scalar:
                     nc.scalar.activation(dst[:, h * HALF : (h + 1) * HALF], src, ACT.Copy, scale=scale)
                 else:
                     nc.vector.tensor_copy(dst[:, h * HALF : (h + 1) * HALF], src)
 
-        def drain(engine, dst, bank, scale):
-            if engine == "scalar":
+        def drain(on_scalar, dst, bank, scale):
+            if on_scalar:
                 nc.scalar.activation(dst, bank, ACT.Copy, scale=scale)
             else:
                 nc.vector.tensor_scalar(dst, bank, scale, None, ALU.mult)
 
-        def add(engine, dst, left, right):
-            (nc.vector if engine == "vector" else nc.gpsimd).tensor_tensor(dst, left, right, ALU.add)
+        def products(name, first_bank, stationary, moving):
+            banks = []
+            for t in range(PACK):
+                bank = psum.tile([P, S], F32, name="%s_bank%d" % (name, t), tag="bank%d" % (first_bank + t))
+                cols = slice(t * P, (t + 1) * P)
+                nc.tensor.matmul_mx(
+                    out=bank[:],
+                    lhsT=stationary[0][:, cols].bitcast(FP8X4),
+                    lhsT_scale=stationary[1][:, cols],
+                    rhs=moving[0][:].bitcast(FP8X4),
+                    rhs_scale=moving[1][:],
+                    start=True,
+                    stop=True,
+                )
+                banks.append(bank)
+            return banks
 
-        def product(bank, cols, lhs, t, rhs):
-            m = slice(t * P, (t + 1) * P)
-            nc.tensor.matmul_mx(
-                out=bank[:, cols], lhsT=lhs[0][:, m].bitcast(FP8X4), lhsT_scale=lhs[1][:, m],
-                rhs=rhs[0][:].bitcast(FP8X4), rhs_scale=rhs[1][:], start=True, stop=True,
-            )
-
-        def weave(name, left, right, op):
-            woven = []
+        def weave_and_quantise(name, left, right, op):
+            woven = [sbuf("%s_woven%d" % (name, h), PACK * HALF, BF16, "woven%d" % h) for h in range(2)]
             for h in range(2):
-                dst = keep.tile([P, HALF * PACK], BF16, name="%s_woven%d" % (name, h), tag="%s_woven%d" % (name, h), align_bytes=64)
                 views = [
                     src[:].rearrange("p (t s) -> p t s", t=PACK)[:, :, h * HALF : (h + 1) * HALF].rearrange("p t (c i) -> p c t i", i=2)
                     for src in (left, right)
                 ]
-                nc.vector.tensor_tensor(dst[:].rearrange("p (c i t) -> p c t i", i=2, t=PACK), views[0], views[1], op)
-                woven.append(dst)
-            packed = []
+                nc.vector.tensor_tensor(woven[h][:].rearrange("p (c i t) -> p c t i", i=2, t=PACK), views[0], views[1], op)
+            codes = sbuf(name + "_codes", S, U32)
+            scales = sbuf(name + "_scales", S, U8)
             for h in range(2):
-                codes = keep.tile([P, HALF], U32, name="%s_codes%d" % (name, h), align_bytes=64)
-                scales = keep.tile([P, HALF], U8, name="%s_scales%d" % (name, h), align_bytes=64)
-                nc.vector.quantize_mx(out=codes[:].bitcast(FP8X4), scales=scales[:], in_=woven[h][:])
-                packed.append((codes, scales))
-            return packed
+                cols = slice(h * HALF, (h + 1) * HALF)
+                nc.vector.quantize_mx(out=codes[:, cols].bitcast(FP8X4), scales=scales[:, cols], in_=woven[h][:])
+            return codes, scales
 
-        ident = keep.tile([P, P], F32, name="ident")
-        make_identity(nc, ident[:])
-        w_bf = keep.tile([P, PACK * S], BF16, name="w_bf", align_bytes=64)
+        w_bf = sbuf("w_bf", PACK * S, BF16)
         w_view = w_bf[:].rearrange("p (t m j) -> p m t j", t=PACK, j=PACK)
         for h, copy in enumerate((nc.vector.tensor_copy, nc.scalar.copy)):
             copy(w_view[:, h * P // 2 : (h + 1) * P // 2], w_raw[h][:].rearrange("p j (m t) -> p m t j", t=PACK))
         xq_scales = pick("xq_scales", x_bytes, offs_l, False)
-        w_codes = keep.tile([P, S], U32, name="w_codes", align_bytes=64)
-        w_scales = keep.tile([P, S], U8, name="w_scales", align_bytes=64)
+        w_codes = sbuf("w_codes", S, U32)
+        w_scales = sbuf("w_scales", S, U8)
         nc.vector.quantize_mx(out=w_codes[:].bitcast(FP8X4), scales=w_scales[:], in_=w_bf[:])
-        xq = (pick("xq_codes", x_codes, offs_l, False), xq_scales)
-        y_banks = [psum.tile([P, S], F32, name="y_bank%d" % t, tag="bank%d" % t) for t in range(PACK)]
-        for t in range(PACK):
-            product(y_banks[t], slice(0, S), (w_codes, w_scales), t, xq)
-        xb_scales = pick("xb_scales", x_bytes, cb_l, True, tag="xq_scales")
-        xb = (pick("xb_codes", x_codes, cb_l, True), xb_scales)
+        xq_codes = pick("xq_codes", x_codes, offs_l, False)
+        y_banks = products("y", 0, (w_codes, w_scales), (xq_codes, xq_scales))
+        xb_scales = pick("xb_scales", x_bytes, cb_l, True)
+        xb_codes = pick("xb_codes", x_codes, cb_l, True)
 
-        y2 = tiles("y2", F32)
-        pa = tiles("pa", BF16)
-        pb = tiles("pb", BF16)
-        hi = tiles("hi", BF16)
-        lo = keep.tile([P, PACK * S], BF16, name="lo", align_bytes=64)
-        mid = keep.tile([P, PACK * S], BF16, name="mid", align_bytes=64)
+        y1, y2, half_n1 = four("y1", F32), four("y2", F32), four("half_n1", F32)
+        st = sbuf("st", PACK * S, F32)
         for t in range(PACK):
-            drain(("scalar", "scalar", "scalar", "scalar")[t], y2[t][:], y_banks[t][:], gain2[:, t : t + 1])
-            fetch("scalar", pb[t], y2[t][:], n4_l)
-            fetch(("vector", "vector", "vector", "scalar")[t], pa[t], y2[t][:], n3_l)
+            drain(True, y1[t][:], y_banks[t][:], gain1[:, t : t + 1])
+            drain(False, y2[t][:], y_banks[t][:], gain2[:, t : t + 1])
+            fetch(True, half_n1[t], y1[t][:], n1_l, scale=0.5)
+            nc.gpsimd.tensor_tensor(part(st, t), y1[t][:], half_n1[t][:], ALU.add)
+
+        pa, pb, hi = four("pa", BF16), four("pb", BF16), four("hi", BF16)
+        lo, mid = sbuf("lo", PACK * S, BF16), sbuf("mid", PACK * S, BF16)
+        for t in range(PACK):
+            fetch(False, pa[t], y2[t][:], n3_l)
+        for t in range(PACK):
+            fetch(True, pb[t], y2[t][:], n4_l)
             nc.vector.tensor_tensor(hi[t][:], pa[t][:], pb[t][:], ALU.max)
-            nc.vector.tensor_tensor(plane(lo, t), pa[t][:], pb[t][:], ALU.min)
-            nc.vector.tensor_tensor(plane(mid, t), hi[t][:], y2[t][:], ALU.min)
-        z2 = weave("z2", lo, mid, ALU.max)
-        b_banks = [psum.tile([P, S], F32, name="b_bank%d" % t, tag="bank%d" % (PACK + t)) for t in range(PACK)]
-        for t in range(PACK):
-            for h in range(2):
-                product(b_banks[t], slice(h * HALF, (h + 1) * HALF), xb, t, z2[h])
+            nc.vector.tensor_tensor(part(lo, t), pa[t][:], pb[t][:], ALU.min)
+            nc.vector.tensor_tensor(part(mid, t), hi[t][:], y2[t][:], ALU.min)
+        b_banks = products("b", PACK, (xb_codes, xb_scales), weave_and_quantise("z2", lo, mid, ALU.max))
 
-        y1 = tiles("y1", F32)
-        g1 = tiles("g1", F32)
-        st = keep.tile([P, PACK * S], F32, name="st", align_bytes=64)
-        g2 = keep.tile([P, PACK * S], F32, name="g2", align_bytes=64)
+        st_n2 = sbuf("st_n2", PACK * S, F32)
         for t in range(PACK):
-            drain(("scalar", "scalar", "scalar", "scalar")[t], y1[t][:], y_banks[t][:], gain1[:, t : t + 1])
-            fetch("scalar", g1[t], y1[t][:], n1_l, scale=0.5)
-            add(("vector", "vector", "vector", "vector")[t], plane(st, t), y1[t][:], g1[t][:])
-        b = tiles("b", F32)
+            fetch(True, part(st_n2, t), part(st, t), n2_l)
+        xa_codes = pick("xa_codes", x_codes, ca_l, True, tag="mid")
+        xa_scales = pick("xa_scales", x_bytes, ca_l, True, tag="lo")
+        b = four("b", F32)
         for t in range(PACK):
-            drain(("scalar", "scalar", "scalar", "scalar")[t], b[t][:], b_banks[t][:], 0.03125)
-        for t in range(PACK):
-            fetch(("vector", "vector", "scalar", "scalar")[t], plane(g2, t), plane(st, t), n2_l)
-        xa = (pick("xa_codes", x_codes, ca_l, True, tag="z2_woven1"), pick("xa_scales", x_bytes, ca_l, True, tag="xq_scales"))
-        z = weave("z", st, g2, ALU.subtract)
-        a_banks = [psum.tile([P, S], F32, name="a_bank%d" % t, tag="bank%d" % t) for t in range(PACK)]
-        for t in range(PACK):
-            for h in range(2):
-                product(a_banks[t], slice(h * HALF, (h + 1) * HALF), xa, t, z[h])
+            drain(True, b[t][:], b_banks[t][:], SCORE_SCALE)
+        a_banks = products("a", 0, (xa_codes, xa_scales), weave_and_quantise("z", st, st_n2, ALU.subtract))
 
-        g6 = tiles("g6", F32)[: PACK - 1] + [keep.tile([P, S], F32, name="g6_last", tag="z_woven1", align_bytes=64)]
-        th = tiles("th", F32)
-        a = tiles("a", F32)
-        g5 = tiles("g5", F32)
-        v = tiles("v", F32)
-        res = tiles("res", F32)
-        gates = []
+        b_n6 = four("b_n6", F32, {2: "st_n2", 3: "st"})
+        u = four("u", F32, {0: "woven0", 1: "woven1"})
+        for t in range(PACK):
+            fetch(t < N6_ON_SCALAR, b_n6[t], b[t][:], n6_l)
+            nc.gpsimd.tensor_tensor(u[t][:], b[t][:], b_n6[t][:], ALU.add)
+        a = four("a", F32)
+        for t in range(PACK):
+            drain(t < A_OUT_ON_SCALAR, a[t][:], a_banks[t][:], SCORE_SCALE)
+        tanh_u, a_n5, v, res = four("tanh_u", F32), four("a_n5", F32), four("v", F32), four("res", F32)
         out_rows = out.rearrange("(p t) s -> p t s", t=PACK)
-        blocks = [slice(c * P, (c + 1) * P) for c in range(S // P)]
-
-        def gate_of(t, engine):
-            fetch(engine, g6[t], b[t][:], n6_l)
-            turned = psum.tile([P, S], F32, name="turned%d" % t, tag="bank%d" % (PACK + t))
-            for cols in blocks:
-                nc.tensor.matmul(turned[:, cols], lhsT=b[t][:, cols], rhs=ident[:], is_transpose=True, start=True, stop=False)
-                nc.tensor.matmul(turned[:, cols], lhsT=g6[t][:, cols], rhs=ident[:], is_transpose=True, start=False, stop=True)
-            nc.scalar.activation(th[t][:], turned[:], ACT.Tanh)
-            gate = psum.tile([P, S], F32, name="gate%d" % t, tag="bank%d" % (PACK + t))
-            for cols in blocks:
-                nc.tensor.transpose(gate[:, cols], th[t][:, cols], ident[:])
-            gates.append(gate)
-
-        for t in range(PACK - 1):
-            gate_of(t, ("scalar", "scalar", "scalar", "vector")[t])
         for t in range(PACK):
-            drain(("vector", "vector", "vector", "vector")[t], a[t][:], a_banks[t][:], 0.03125)
-        gate_of(PACK - 1, ("scalar", "scalar", "scalar", "vector")[PACK - 1])
-        for t in range(PACK):
-            fetch("scalar", g5[t], a[t][:], n5_l)
-            for cols in ([slice(0, S)] if t < PACK - 1 else [slice(0, HALF), slice(HALF, S)]):
-                add(("vector", "vector", "vector", "vector")[t], v[t][:, cols], a[t][:, cols], g5[t][:, cols])
-                nc.vector.scalar_tensor_tensor(res[t][:, cols], gates[t][:, cols], 1.0, v[t][:, cols], ALU.add, ALU.mult)
+            nc.scalar.activation(tanh_u[t][:], u[t][:], ACT.Tanh)
+            fetch(True, a_n5[t], a[t][:], n5_l)
+            pieces = 2 if t == PACK - 1 else 1
+            for i in range(pieces):
+                cols = slice(i * S // pieces, (i + 1) * S // pieces)
+                nc.vector.tensor_tensor(v[t][:, cols], a[t][:, cols], a_n5[t][:, cols], ALU.add)
+                nc.vector.scalar_tensor_tensor(res[t][:, cols], tanh_u[t][:, cols], 1.0, v[t][:, cols], ALU.add, ALU.mult)
                 nc.sync.dma_start(out_rows[:, t, cols], res[t][:, cols])

@@ -19,6 +19,7 @@ P = 128
 PACK = 4
 HALF = S // 2
 GROUP = 16
+GAINS_ON_GPSIMD = 2
 N6_ON_SCALAR = 2
 A_OUT_ON_SCALAR = 1
 SCORE_SCALE = 0.0625 * 0.5
@@ -140,15 +141,25 @@ def tile_picked_twocdtriebhopmed_none_p_kernel(tc, x_words, x_scales, w1, gs, gs
         y1, y2, half_n1 = four("y1", F32), four("y2", F32), four("half_n1", F32)
         st = sbuf("st", PACK * S, F32)
         for t in range(PACK):
-            drain(True, y1[t][:], y_banks[t][:], gain1[:, t : t + 1])
-            drain(False, y2[t][:], y_banks[t][:], gain2[:, t : t + 1])
+            once = t < GAINS_ON_GPSIMD
+            drain(True, y1[t][:], y_banks[t][:], 1.0 if once else gain1[:, t : t + 1])
+            if once:
+                nc.gpsimd.tensor_scalar(y2[t][:], y1[t][:], gain2[:, t : t + 1], 0.0, ALU.mult, ALU.add)
+            else:
+                drain(False, y2[t][:], y_banks[t][:], gain2[:, t : t + 1])
             fetch(True, half_n1[t], y1[t][:], n1_l, scale=0.5)
-            nc.gpsimd.tensor_tensor(part(st, t), y1[t][:], half_n1[t][:], ALU.add)
+            if once:
+                y_sum = sbuf("y_sum%d" % t, S, F32)
+                nc.gpsimd.tensor_tensor(y_sum[:], y1[t][:], half_n1[t][:], ALU.add)
+                nc.gpsimd.tensor_scalar(part(st, t), y_sum[:], gain1[:, t : t + 1], 0.0, ALU.mult, ALU.add)
+            else:
+                nc.gpsimd.tensor_tensor(part(st, t), y1[t][:], half_n1[t][:], ALU.add)
 
         pa, pb, hi = four("pa", BF16), four("pb", BF16), four("hi", BF16)
         lo, mid = sbuf("lo", PACK * S, BF16), sbuf("mid", PACK * S, BF16)
         for t in range(PACK):
             fetch(False, pa[t], y2[t][:], n3_l)
+        xa_codes = pick("xa_codes", x_codes, ca_l, True, tag=None)
         for t in range(PACK):
             fetch(True, pb[t], y2[t][:], n4_l)
             nc.vector.tensor_tensor(hi[t][:], pa[t][:], pb[t][:], ALU.max)
@@ -159,22 +170,27 @@ def tile_picked_twocdtriebhopmed_none_p_kernel(tc, x_words, x_scales, w1, gs, gs
         st_n2 = sbuf("st_n2", PACK * S, F32)
         for t in range(PACK):
             fetch(True, part(st_n2, t), part(st, t), n2_l)
-        xa_codes = pick("xa_codes", x_codes, ca_l, True, tag="mid")
         xa_scales = pick("xa_scales", x_bytes, ca_l, True, tag="lo")
-        b = four("b", F32)
-        for t in range(PACK):
+        b = four("b", F32, {3: "st"})
+        for t in range(PACK - 1):
             drain(True, b[t][:], b_banks[t][:], SCORE_SCALE)
         a_banks = products("a", 0, (xa_codes, xa_scales), weave_and_quantise("z", st, st_n2, ALU.subtract))
 
-        b_n6 = four("b_n6", F32, {2: "st_n2", 3: "st"})
+        b_n6 = four("b_n6", F32, {2: "st_n2"})
         u = four("u", F32, {0: "woven0", 1: "woven1"})
-        for t in range(PACK):
+
+        def sum_b(t):
             fetch(t < N6_ON_SCALAR, b_n6[t], b[t][:], n6_l)
             nc.gpsimd.tensor_tensor(u[t][:], b[t][:], b_n6[t][:], ALU.add)
+
         a = four("a", F32)
+        for t in range(3):
+            sum_b(t)
         for t in range(PACK):
             drain(t < A_OUT_ON_SCALAR, a[t][:], a_banks[t][:], SCORE_SCALE)
-        tanh_u, a_n5, v, res = four("tanh_u", F32), four("a_n5", F32), four("v", F32), four("res", F32)
+        drain(False, b[3][:], b_banks[3][:], SCORE_SCALE)
+        sum_b(3)
+        tanh_u, a_n5, v, res = four("tanh_u", F32), four("a_n5", F32), four("v", F32, {3: "v1"}), four("res", F32)
         out_rows = out.rearrange("(p t) s -> p t s", t=PACK)
         for t in range(PACK):
             nc.scalar.activation(tanh_u[t][:], u[t][:], ACT.Tanh)
@@ -182,6 +198,6 @@ def tile_picked_twocdtriebhopmed_none_p_kernel(tc, x_words, x_scales, w1, gs, gs
             pieces = 2 if t == PACK - 1 else 1
             for i in range(pieces):
                 cols = slice(i * S // pieces, (i + 1) * S // pieces)
-                nc.vector.tensor_tensor(v[t][:, cols], a[t][:, cols], a_n5[t][:, cols], ALU.add)
+                nc.vector.scalar_tensor_tensor(v[t][:, cols], a_banks[t][:, cols], SCORE_SCALE, a_n5[t][:, cols], ALU.mult, ALU.add)
                 nc.vector.scalar_tensor_tensor(res[t][:, cols], tanh_u[t][:, cols], 1.0, v[t][:, cols], ALU.add, ALU.mult)
                 nc.sync.dma_start(out_rows[:, t, cols], res[t][:, cols])

@@ -19,6 +19,7 @@ P = 128
 PACK = 4
 HALF = S // 2
 GROUP = 16
+LAST = PACK - 1
 GAINS_ON_GPSIMD = 2
 N6_ON_SCALAR = 2
 A_OUT_ON_SCALAR = 1
@@ -56,7 +57,7 @@ def tile_picked_twocdtriebhopmed_none_p_kernel(tc, x_words, x_scales, w1, gs, gs
         w_rows = w1.rearrange("(p j) c -> p j c", j=PACK)
         w_raw = [keep.tile([P, PACK, HALF], F32, name="w_raw%d" % h) for h in range(2)]
         nc.sync.dma_start(w_raw[0][:], w_rows[:, :, :HALF])
-        for q in range(4):
+        for q in range(P // 32):
             nc.sync.dma_start(x_bytes[32 * q : 32 * q + 4, :].bitcast(I32), x_scales[0, 4 * q : 4 * q + 4, :].bitcast(I32))
         offs_l = load_list("offs_l", offs)
         nc.sync.dma_start(w_raw[1][:], w_rows[:, :, HALF:])
@@ -138,28 +139,28 @@ def tile_picked_twocdtriebhopmed_none_p_kernel(tc, x_words, x_scales, w1, gs, gs
         xb_scales = pick("xb_scales", x_bytes, cb_l, True)
         xb_codes = pick("xb_codes", x_codes, cb_l, True)
 
-        y1, y2, half_n1 = four("y1", F32), four("y2", F32), four("half_n1", F32)
+        n1_window, y2, half_n1 = four("n1_window", F32), four("y2", F32), four("half_n1", F32)
         st = sbuf("st", PACK * S, F32)
         for t in range(PACK):
             once = t < GAINS_ON_GPSIMD
-            drain(True, y1[t][:], y_banks[t][:], 1.0 if once else gain1[:, t : t + 1])
+            drain(True, n1_window[t][:], y_banks[t][:], 1.0 if once else gain1[:, t : t + 1])
             if once:
-                nc.gpsimd.tensor_scalar(y2[t][:], y1[t][:], gain2[:, t : t + 1], 0.0, ALU.mult, ALU.add)
+                nc.gpsimd.tensor_scalar(y2[t][:], n1_window[t][:], gain2[:, t : t + 1], 0.0, ALU.mult, ALU.add)
             else:
                 drain(False, y2[t][:], y_banks[t][:], gain2[:, t : t + 1])
-            fetch(True, half_n1[t], y1[t][:], n1_l, scale=0.5)
+            fetch(True, half_n1[t], n1_window[t][:], n1_l, scale=0.5)
             if once:
                 y_sum = sbuf("y_sum%d" % t, S, F32)
-                nc.gpsimd.tensor_tensor(y_sum[:], y1[t][:], half_n1[t][:], ALU.add)
+                nc.gpsimd.tensor_tensor(y_sum[:], n1_window[t][:], half_n1[t][:], ALU.add)
                 nc.gpsimd.tensor_scalar(part(st, t), y_sum[:], gain1[:, t : t + 1], 0.0, ALU.mult, ALU.add)
             else:
-                nc.gpsimd.tensor_tensor(part(st, t), y1[t][:], half_n1[t][:], ALU.add)
+                nc.gpsimd.tensor_tensor(part(st, t), n1_window[t][:], half_n1[t][:], ALU.add)
 
         pa, pb, hi = four("pa", BF16), four("pb", BF16), four("hi", BF16)
         lo, mid = sbuf("lo", PACK * S, BF16), sbuf("mid", PACK * S, BF16)
         for t in range(PACK):
             fetch(False, pa[t], y2[t][:], n3_l)
-        xa_codes = pick("xa_codes", x_codes, ca_l, True, tag=None)
+        xa_codes = pick("xa_codes", x_codes, ca_l, True)
         for t in range(PACK):
             fetch(True, pb[t], y2[t][:], n4_l)
             nc.vector.tensor_tensor(hi[t][:], pa[t][:], pb[t][:], ALU.max)
@@ -171,12 +172,12 @@ def tile_picked_twocdtriebhopmed_none_p_kernel(tc, x_words, x_scales, w1, gs, gs
         for t in range(PACK):
             fetch(True, part(st_n2, t), part(st, t), n2_l)
         xa_scales = pick("xa_scales", x_bytes, ca_l, True, tag="lo")
-        b = four("b", F32, {3: "st"})
-        for t in range(PACK - 1):
+        b = four("b", F32, {LAST: "st"})
+        for t in range(LAST):
             drain(True, b[t][:], b_banks[t][:], SCORE_SCALE)
         a_banks = products("a", 0, (xa_codes, xa_scales), weave_and_quantise("z", st, st_n2, ALU.subtract))
 
-        b_n6 = four("b_n6", F32, {2: "st_n2"})
+        b_n6 = four("b_n6", F32, {N6_ON_SCALAR: "st_n2"})
         u = four("u", F32, {0: "woven0", 1: "woven1"})
 
         def sum_b(t):
@@ -184,20 +185,24 @@ def tile_picked_twocdtriebhopmed_none_p_kernel(tc, x_words, x_scales, w1, gs, gs
             nc.gpsimd.tensor_tensor(u[t][:], b[t][:], b_n6[t][:], ALU.add)
 
         a = four("a", F32)
-        for t in range(3):
+        for t in range(LAST):
             sum_b(t)
         for t in range(PACK):
             drain(t < A_OUT_ON_SCALAR, a[t][:], a_banks[t][:], SCORE_SCALE)
-        drain(False, b[3][:], b_banks[3][:], SCORE_SCALE)
-        sum_b(3)
-        tanh_u, a_n5, v, res = four("tanh_u", F32), four("a_n5", F32), four("v", F32, {3: "v1"}), four("res", F32)
+        drain(False, b[LAST][:], b_banks[LAST][:], SCORE_SCALE)
+        sum_b(LAST)
+        tanh_u, a_n5, v, res = four("tanh_u", F32), four("a_n5", F32), four("v", F32, {LAST: "v1"}), four("res", F32)
         out_rows = out.rearrange("(p t) s -> p t s", t=PACK)
         for t in range(PACK):
-            nc.scalar.activation(tanh_u[t][:], u[t][:], ACT.Tanh)
+            last = t == LAST
+            pieces = [slice(0, HALF), slice(HALF, S)] if last else [slice(0, S)]
+            if not last:
+                nc.scalar.activation(tanh_u[t][:], u[t][:], ACT.Tanh)
             fetch(True, a_n5[t], a[t][:], n5_l)
-            pieces = 2 if t == PACK - 1 else 1
-            for i in range(pieces):
-                cols = slice(i * S // pieces, (i + 1) * S // pieces)
+            for cols in pieces:
                 nc.vector.scalar_tensor_tensor(v[t][:, cols], a_banks[t][:, cols], SCORE_SCALE, a_n5[t][:, cols], ALU.mult, ALU.add)
+            for cols in pieces:
+                if last:
+                    nc.scalar.activation(tanh_u[t][:, cols], u[t][:, cols], ACT.Tanh)
                 nc.vector.scalar_tensor_tensor(res[t][:, cols], tanh_u[t][:, cols], 1.0, v[t][:, cols], ALU.add, ALU.mult)
                 nc.sync.dma_start(out_rows[:, t, cols], res[t][:, cols])

from contextlib import ExitStack

import concourse.mybir as mybir

K, T, S = 512, 2048, 512
FLOPS = 3 * 2 * K * S * S

F32 = mybir.dt.float32
BF16 = mybir.dt.bfloat16
I32 = mybir.dt.int32
U32 = mybir.dt.uint32
U16 = mybir.dt.uint16
U8 = mybir.dt.uint8
FP8X4 = mybir.dt.float8_e4m3fn_x4
ALU = mybir.AluOpType
ACT = mybir.ActivationFunctionType

P = 128
PACK = 4
HALF = S // 2
GROUP = 16
LAST = PACK - 1
GAINS_ON_GPSIMD = 2
N6_ON_SCALAR = 2
A_OUT_ON_SCALAR = 1
SCORE_SCALE = 0.0625 * 0.5


def tile_picked_twocdtriebhopmed_none_p_kernel(tc, x_words, x_scales, w1, gs, gs2, offs, n1, n2, n3, n4, ca, cb, n5, n6, out):
    nc = tc.nc
    with ExitStack() as ctx:
        lists = ctx.enter_context(tc.tile_pool(name="lists", bufs=1))
        keep = ctx.enter_context(tc.tile_pool(name="keep", bufs=1))
        psum = ctx.enter_context(tc.psum_pool(name="psum", bufs=1))

        def sbuf(name, width, dtype, tag=None):
            return keep.tile([P, width], dtype, name=name, tag=tag or name, align_bytes=64)

        def four(name, dtype, tags=None):
            return [sbuf("%s%d" % (name, t), S, dtype, (tags or {}).get(t)) for t in range(PACK)]

        def part(tile, t):
            return tile[:, t * S : (t + 1) * S]

        def load_list(name, src):
            tile = lists.tile([P, S // GROUP], U16, name=name)
            nc.sync.dma_start(tile[:], src)
            return tile

        def load_gain(name, src):
            tile = sbuf(name, PACK, F32)
            nc.sync.dma_start(tile[:], src.rearrange("(p t) o -> p (t o)", t=PACK))
            return tile

        x_bytes = sbuf("x_bytes", T, U8)
        nc.vector.memset(x_bytes[:].bitcast(I32), 0)
        w_rows = w1.rearrange("(p j) c -> p j c", j=PACK)
        w_raw = [keep.tile([P, PACK, HALF], F32, name="w_raw%d" % h) for h in range(2)]
        nc.sync.dma_start(w_raw[0][:], w_rows[:, :, :HALF])
        for q in range(P // 32):
            nc.sync.dma_start(x_bytes[32 * q : 32 * q + 4, :].bitcast(I32), x_scales[0, 4 * q : 4 * q + 4, :].bitcast(I32))
        offs_l = load_list("offs_l", offs)
        nc.sync.dma_start(w_raw[1][:], w_rows[:, :, HALF:])
        x_codes = sbuf("x_codes", T, U32)
        nc.sync.dma_start(x_codes[:].bitcast(I32), x_words[0].rearrange("p n t -> p (n t)").bitcast(I32))
        cb_l = load_list("cb_l", cb)
        gain1 = load_gain("gain1", gs)
        n1_l = load_list("n1_l", n1)
        gain2 = load_gain("gain2", gs2)
        n3_l = load_list("n3_l", n3)
        n4_l = load_list("n4_l", n4)
        n2_l = load_list("n2_l", n2)
        ca_l = load_list("ca_l", ca)
        n6_l = load_list("n6_l", n6)
        n5_l = load_list("n5_l", n5)

        def pick(name, table, offsets, dealt, tag=None):
            dst = sbuf(name, S, table.dtype, tag)
            view = dst[:].rearrange("p (t m) -> p m t", t=PACK) if dealt else dst[:]
            nc.vector.tensor_copy(view, table[:].indirect(offsets[:]))
            return dst

        def fetch(on_scalar, dst, window, offsets, scale=1.0):
            for h in range(2):
                src = window.indirect(offsets[:, h * HALF // GROUP : (h + 1) * HALF // GROUP])
                if on_scalar:
                    nc.scalar.activation(dst[:, h * HALF : (h + 1) * HALF], src, ACT.Copy, scale=scale)
                else:
                    nc.vector.tensor_copy(dst[:, h * HALF : (h + 1) * HALF], src)

        def drain(on_scalar, dst, bank, scale):
            if on_scalar:
                nc.scalar.activation(dst, bank, ACT.Copy, scale=scale)
            else:
                nc.vector.tensor_scalar(dst, bank, scale, None, ALU.mult)

        def products(name, first_bank, stationary, moving):
            banks = []
            for t in range(PACK):
                bank = psum.tile([P, S], F32, name="%s_bank%d" % (name, t), tag="bank%d" % (first_bank + t))
                cols = slice(t * P, (t + 1) * P)
                nc.tensor.matmul_mx(
                    out=bank[:],
                    lhsT=stationary[0][:, cols].bitcast(FP8X4),
                    lhsT_scale=stationary[1][:, cols],
                    rhs=moving[0][:].bitcast(FP8X4),
                    rhs_scale=moving[1][:],
                    start=True,
                    stop=True,
                )
                banks.append(bank)
            return banks

        def weave_and_quantise(name, left, right, op):
            woven = [sbuf("%s_woven%d" % (name, h), PACK * HALF, BF16, "woven%d" % h) for h in range(2)]
            for h in range(2):
                views = [
                    src[:].rearrange("p (t s) -> p t s", t=PACK)[:, :, h * HALF : (h + 1) * HALF].rearrange("p t (c i) -> p c t i", i=2)
                    for src in (left, right)
                ]
                nc.vector.tensor_tensor(woven[h][:].rearrange("p (c i t) -> p c t i", i=2, t=PACK), views[0], views[1], op)
            codes = sbuf(name + "_codes", S, U32)
            scales = sbuf(name + "_scales", S, U8)
            for h in range(2):
                cols = slice(h * HALF, (h + 1) * HALF)
                nc.vector.quantize_mx(out=codes[:, cols].bitcast(FP8X4), scales=scales[:, cols], in_=woven[h][:])
            return codes, scales

        w_bf = sbuf("w_bf", PACK * S, BF16)
        w_view = w_bf[:].rearrange("p (t m j) -> p m t j", t=PACK, j=PACK)
        for h, copy in enumerate((nc.vector.tensor_copy, nc.scalar.copy)):
            copy(w_view[:, h * P // 2 : (h + 1) * P // 2], w_raw[h][:].rearrange("p j (m t) -> p m t j", t=PACK))
        xq_scales = pick("xq_scales", x_bytes, offs_l, False)
        w_codes = sbuf("w_codes", S, U32)
        w_scales = sbuf("w_scales", S, U8)
        nc.vector.quantize_mx(out=w_codes[:].bitcast(FP8X4), scales=w_scales[:], in_=w_bf[:])
        xq_codes = pick("xq_codes", x_codes, offs_l, False)
        y_banks = products("y", 0, (w_codes, w_scales), (xq_codes, xq_scales))
        xb_scales = pick("xb_scales", x_bytes, cb_l, True)
        xb_codes = pick("xb_codes", x_codes, cb_l, True)

        n1_window, y2, half_n1 = four("n1_window", F32), four("y2", F32), four("half_n1", F32)
        st = sbuf("st", PACK * S, F32)
        for t in range(PACK):
            once = t < GAINS_ON_GPSIMD
            drain(True, n1_window[t][:], y_banks[t][:], 1.0 if once else gain1[:, t : t + 1])
            if once:
                nc.gpsimd.tensor_scalar(y2[t][:], n1_window[t][:], gain2[:, t : t + 1], 0.0, ALU.mult, ALU.add)
            else:
                drain(False, y2[t][:], y_banks[t][:], gain2[:, t : t + 1])
            fetch(True, half_n1[t], n1_window[t][:], n1_l, scale=0.5)
            if once:
                y_sum = sbuf("y_sum%d" % t, S, F32)
                nc.gpsimd.tensor_tensor(y_sum[:], n1_window[t][:], half_n1[t][:], ALU.add)
                nc.gpsimd.tensor_scalar(part(st, t), y_sum[:], gain1[:, t : t + 1], 0.0, ALU.mult, ALU.add)
            else:
                nc.gpsimd.tensor_tensor(part(st, t), n1_window[t][:], half_n1[t][:], ALU.add)

        pa, pb, hi = four("pa", BF16), four("pb", BF16), four("hi", BF16)
        lo, mid = sbuf("lo", PACK * S, BF16), sbuf("mid", PACK * S, BF16)
        for t in range(PACK):
            fetch(False, pa[t], y2[t][:], n3_l)
        xa_codes = pick("xa_codes", x_codes, ca_l, True)
        for t in range(PACK):
            fetch(True, pb[t], y2[t][:], n4_l)
            nc.vector.tensor_tensor(hi[t][:], pa[t][:], pb[t][:], ALU.max)
            nc.vector.tensor_tensor(part(lo, t), pa[t][:], pb[t][:], ALU.min)
            nc.vector.tensor_tensor(part(mid, t), hi[t][:], y2[t][:], ALU.min)
        b_banks = products("b", PACK, (xb_codes, xb_scales), weave_and_quantise("z2", lo, mid, ALU.max))

        st_n2 = sbuf("st_n2", PACK * S, F32)
        for t in range(PACK):
            fetch(True, part(st_n2, t), part(st, t), n2_l)
        xa_scales = pick("xa_scales", x_bytes, ca_l, True, tag="lo")
        b = four("b", F32, {LAST: "st"})
        for t in range(LAST):
            drain(True, b[t][:], b_banks[t][:], SCORE_SCALE)
        a_banks = products("a", 0, (xa_codes, xa_scales), weave_and_quantise("z", st, st_n2, ALU.subtract))

        b_n6 = four("b_n6", F32, {N6_ON_SCALAR: "st_n2"})
        u = four("u", F32, {0: "woven0", 1: "woven1"})

        def sum_b(t):
            fetch(t < N6_ON_SCALAR, b_n6[t], b[t][:], n6_l)
            nc.gpsimd.tensor_tensor(u[t][:], b[t][:], b_n6[t][:], ALU.add)

        a = four("a", F32)
        for t in range(LAST):
            sum_b(t)
        for t in range(PACK):
            drain(t < A_OUT_ON_SCALAR, a[t][:], a_banks[t][:], SCORE_SCALE)
        drain(False, b[LAST][:], b_banks[LAST][:], SCORE_SCALE)
        sum_b(LAST)
        tanh_u, a_n5, v, res = four("tanh_u", F32), four("a_n5", F32), four("v", F32, {LAST: "v1"}), four("res", F32)
        out_rows = out.rearrange("(p t) s -> p t s", t=PACK)
        for t in range(PACK):
            last = t == LAST
            pieces = [slice(0, HALF), slice(HALF, S)] if last else [slice(0, S)]
            if not last:
                nc.scalar.activation(tanh_u[t][:], u[t][:], ACT.Tanh)
            fetch(True, a_n5[t], a[t][:], n5_l)
            for cols in pieces:
                nc.vector.scalar_tensor_tensor(v[t][:, cols], a_banks[t][:, cols], SCORE_SCALE, a_n5[t][:, cols], ALU.mult, ALU.add)
            for cols in pieces:
                if last:
                    nc.scalar.activation(tanh_u[t][:, cols], u[t][:, cols], ACT.Tanh)
                nc.vector.scalar_tensor_tensor(res[t][:, cols], tanh_u[t][:, cols], 1.0, v[t][:, cols], ALU.add, ALU.mult)
                nc.sync.dma_start(out_rows[:, t, cols], res[t][:, cols])
